import numpy as np
import ml_dtypes


def mxq(x, axis, fmt="e4m3"):
    dtype, down = {"e4m3": (ml_dtypes.float8_e4m3fn, 7), "e5m2": (ml_dtypes.float8_e5m2, 14)}[fmt]
    v = np.moveaxis(np.asarray(x, np.float32).astype(ml_dtypes.bfloat16).astype(np.float64), axis, -1)
    blocks = v.reshape(v.shape[:-1] + (-1, 32))
    amax = np.abs(blocks).max(-1, keepdims=True)
    byte = np.maximum(np.where(amax > 0, np.frexp(amax)[1] - 1 + 127, 0) - down, 1)
    scale = np.exp2(byte - 127.0)
    codes = (blocks / scale).astype(np.float32).astype(dtype).astype(np.float64)
    return np.moveaxis((codes * scale).reshape(v.shape), -1, axis)


WIDE = False


def mx_kscale(k):
    if not WIDE:
        return np.ones(k)
    levels = np.array([10, -10, 5, -5, 0])
    if k % 512:
        return np.exp2(np.random.permutation(np.resize(levels, k // 32))).repeat(32)
    a = np.empty((k // 512, 16))
    for p in range(k // 512):
        a[p, :8] = np.random.permutation(np.resize(levels, 8))
        for g in range(8):
            far = levels[np.abs(levels - a[p, g]) >= 10]
            a[p, g + 8] = far[np.random.randint(len(far))]
    return np.exp2(a.ravel()).repeat(32)


BF16 = ml_dtypes.bfloat16


def bf(x):
    return np.asarray(x, np.float32).astype(BF16)


def f64(x):
    return np.asarray(x).astype(np.float64)


T, D, H, N = 4096, 512, 4, 32
TWO = 2
C = H * TWO * N
SLOTS = N * N


def draw0():
    s = mx_kscale(D)
    t = mx_kscale(SLOTS)
    return {
        "x": bf(np.random.standard_normal((T, D)) * s),
        "wk": bf(np.random.standard_normal((D, C)) * 1.5 / np.sqrt(D) / s[:, None]),
        "slot_gain": bf(np.random.standard_normal(SLOTS) * np.sqrt(SLOTS) * t),
        "values": bf(np.random.standard_normal((SLOTS, D)) * 2.0 / np.sqrt(SLOTS) / t[:, None]),
        "wg": bf(np.random.standard_normal((D, D)) * 1.5 / np.sqrt(D) / s[:, None]),
    }


def softmax(v):
    e = np.exp(v - v.max(-1, keepdims=True))
    return e / e.sum(-1, keepdims=True)


def product_key_weights(sc):
    p = softmax(sc)
    p1 = p[:, :, 0, :]
    p2 = p[:, :, 1, :]
    w = np.sum(p1[:, :, :, None] * p2[:, :, None, :], axis=1)
    return w.reshape(w.shape[0], SLOTS)


def core(x, wk, slot_gain, values, wg):
    xq = mxq(f64(x), 1, "e4m3")
    sc = (xq @ mxq(f64(wk), 0, "e4m3")).reshape(x.shape[0], H, TWO, N)
    w = product_key_weights(sc)
    wg_slots = w * f64(slot_gain)[None, :]
    mem = mxq(wg_slots, 1, "e4m3") @ mxq(f64(values), 0, "e4m3")
    a = xq @ mxq(f64(wg), 0, "e4m3")
    gate = a * (1.0 / (1.0 + np.exp(-a)))
    return mem * gate


def e4m3fn_bytes(y):
    return np.clip(np.asarray(y, np.float64), -448.0, 448.0).astype(np.float32).astype(ml_dtypes.float8_e4m3fn).view(np.uint8)


def e4m3fn_values(b):
    return np.asarray(b, np.uint8).view(ml_dtypes.float8_e4m3fn).astype(np.float64)


def setup_inputs():
    d = draw0()
    x0 = np.asarray(d['x']).astype(np.float64)
    s = (np.max(np.abs(x0), axis=(0,), keepdims=True) / 448.0).astype(np.float32)
    out = {}
    for k, v in d.items():
        if k == 'x':
            out['x_bytes'] = e4m3fn_bytes(x0 / s.astype(np.float64))
            out['x_scale'] = s
        else:
            out[k] = v
    return out


def reference(x_bytes, x_scale, wk, slot_gain, values, wg):
    return core(e4m3fn_values(x_bytes) * x_scale.astype(np.float64), wk, slot_gain, values, wg)

@@ -1,0 +1,398 @@
+from contextlib import ExitStack
+
+import concourse.mybir as mybir
+from concourse.masks import make_identity
+
+F32 = mybir.dt.float32
+BF16 = mybir.dt.bfloat16
+U32 = mybir.dt.uint32
+U8 = mybir.dt.uint8
+FP8 = mybir.dt.float8_e4m3fn
+FP8X4 = mybir.dt.float8_e4m3fn_x4
+ACT = mybir.ActivationFunctionType
+ALU = mybir.AluOpType
+AX = mybir.AxisListType
+
+T, D, H, N = 4096, 512, 4, 32
+C = H * 2 * N
+SLOTS = N * N
+P = 128
+NT = T // P
+
+FLOPS = 2 * T * D * C + 2 * T * SLOTS * D + 2 * T * D * D
+
+V_UNITS = [(0, 0), (0, 1)]
+S_UNITS = [(1, 0), (1, 1), (2, 0)]
+G_UNITS = [(3, 0), (2, 1), (3, 1)]
+
+X_CHUNKS = [(0, 2), (2, 8), (8, 16), (16, 24), (24, 32)]
+
+
+def tile_productkeysoftmemoryplus_t_kernel(
+    tc, x_bytes, x_scale, wk, slot_gain, values, wg, out
+):
+    nc = tc.nc
+    x_view = x_bytes.rearrange("(p n) d -> p n d", n=NT)
+    out_view = out.rearrange("(p n) d -> p n d", n=NT)
+
+    with ExitStack() as ctx:
+        keep = ctx.enter_context(tc.tile_pool(name="keep", bufs=1))
+        work = ctx.enter_context(tc.tile_pool(name="work", bufs=2))
+        psum = ctx.enter_context(tc.psum_pool(name="psum", bufs=1))
+        ctx.enter_context(tc.manual_schedule())
+
+        xraw = []
+        for a, b in X_CHUNKS:
+            xr = keep.tile([P, b - a, D], U8, name="xraw%d" % a, align_bytes=64)
+            xraw.append(xr)
+        scale_sb = keep.tile([P, D], F32, name="scale_sb")
+        wg_raw = keep.tile([P, 4, D], BF16, name="wg_raw")
+        wk_raw = keep.tile([P, 4, C], BF16, name="wk_raw")
+        v_raw = keep.tile([P, 2, 4, D], BF16, name="v_raw")
+        gain_sb = keep.tile([P, 2, 4], BF16, name="gain_sb")
+
+        def load_x(i):
+            a, b = X_CHUNKS[i]
+            nc.sync.dma_start(out=xraw[i][:], in_=x_view[:, a:b, :])
+
+        nc.sync.dma_start(out=scale_sb[:], in_=x_scale.rearrange("o k -> (o k)").partition_broadcast(P))
+        load_x(0)
+        nc.sync.dma_start(out=wg_raw[:], in_=wg.rearrange("(p j) c -> p j c", j=4))
+        load_x(1)
+        nc.sync.dma_start(out=wk_raw[:], in_=wk.rearrange("(p j) c -> p j c", j=4))
+        load_x(2)
+        for g in range(2):
+            nc.sync.dma_start(
+                out=v_raw[:, g, :, :],
+                in_=values[512 * g : 512 * (g + 1), :].rearrange("(p j) c -> p j c", j=4),
+            )
+        nc.sync.dma_start(out=gain_sb[:], in_=slot_gain.rearrange("(g p t) -> p g t", p=P, t=4))
+        load_x(3)
+        load_x(4)
+
+        ident = keep.tile([P, P], F32, name="ident")
+        make_identity(nc, ident[:])
+        warm = keep.tile([P, 1], F32, name="warm")
+        nc.gpsimd.memset(warm[:], 0.0)
+        warm_out = keep.tile([P, 1], F32, name="warm_out")
+        nc.scalar.activation(out=warm_out[:], in_=warm[:], func=ACT.Silu)
+
+        x_codes = keep.tile([P, T], U32, name="x_codes", align_bytes=64)
+        x_planes = keep.tile([P, T], U8, name="x_planes", align_bytes=64)
+        wg_codes = keep.tile([P, D], U32, name="wg_codes", align_bytes=64)
+        wg_planes = keep.tile([P, D], U8, name="wg_planes", align_bytes=64)
+        wk_codes = keep.tile([P, C], U32, name="wk_codes", align_bytes=64)
+        wk_planes = keep.tile([P, C], U8, name="wk_planes", align_bytes=64)
+        v_codes = keep.tile([P, 2, D], U32, name="v_codes", align_bytes=64)
+        v_planes = keep.tile([P, 2, D], U8, name="v_planes", align_bytes=64)
+        gate = keep.tile([P, NT, D], F32, name="gate")
+
+        wg_il = keep.tile([P, D, 4], BF16, name="wg_il", align_bytes=64)
+        nc.scalar.copy(out=wg_il[:], in_=wg_raw[:].rearrange("p j c -> p c j"))
+
+        def wk_copy():
+            wk_il = keep.tile([P, C, 4], BF16, name="wk_il", align_bytes=64)
+            nc.vector.tensor_copy(out=wk_il[:], in_=wk_raw[:].rearrange("p j c -> p c j"))
+            state["wk_il"] = wk_il
+
+        def wk_quant():
+            nc.vector.quantize_mx(
+                out=wk_codes[:].bitcast(FP8X4),
+                scales=wk_planes[:],
+                in_=state["wk_il"][:].rearrange("p c j -> p (c j)"),
+            )
+
+        def v_copy(i):
+            g, b = divmod(i, 2)
+            v_il = work.tile([P, 256, 4], BF16, name="v_il", align_bytes=64)
+            nc.vector.tensor_copy(
+                out=v_il[:],
+                in_=v_raw[:, g, :, 256 * b : 256 * (b + 1)].rearrange("p j c -> p c j"),
+            )
+            state["v_il", i] = v_il
+
+        def v_quant(i):
+            g, b = divmod(i, 2)
+            cols = slice(256 * b, 256 * (b + 1))
+            nc.vector.quantize_mx(
+                out=v_codes[:, g, cols].bitcast(FP8X4),
+                scales=v_planes[:, g, cols],
+                in_=state["v_il", i][:].rearrange("p c j -> p (c j)"),
+            )
+
+        state = {}
+        prep = {3: [wk_copy], 4: [wk_quant]}
+        for i in range(4):
+            prep.setdefault(6 + 2 * i, []).append(lambda i=i: v_copy(i))
+            prep.setdefault(7 + 2 * i, []).append(lambda i=i: v_quant(i))
+
+        def x_product(q):
+            xb = work.tile([P, 2, D], BF16, name="xb", align_bytes=64)
+            for s in range(2):
+                n = 2 * q + s
+                i = [k for k, (a, b) in enumerate(X_CHUNKS) if a <= n < b][0]
+                nc.vector.tensor_tensor(
+                    out=xb[:, s, :],
+                    in0=xraw[i][:, n - X_CHUNKS[i][0], :].bitcast(FP8),
+                    in1=scale_sb[:],
+                    op=ALU.mult,
+                )
+            state["xb", q] = xb
+
+        def x_transpose(q):
+            words = state["xb", q][:].rearrange("p s d -> p (s d)").bitcast(F32)
+            xt = psum.tile([P, 2, 2, P], F32, name="xt", tag="sc", bufs=2)
+            for s in range(2):
+                for u in range(2):
+                    nc.tensor.transpose(
+                        xt[:, s, u, :], words[:, 256 * s + u : 256 * (s + 1) : 2], ident[:]
+                    )
+            state["xt", q] = xt
+
+        def x_copy(q):
+            xg = work.tile([P, 2 * P, 4], BF16, name="xg", align_bytes=64)
+            nc.scalar.copy(
+                out=xg[:].rearrange("p k t -> p (k t)").bitcast(F32).rearrange(
+                    "p (s k u) -> p s k u", s=2, u=2
+                ),
+                in_=state["xt", q][:].rearrange("p s u k -> p s k u"),
+            )
+            state["xg", q] = xg
+
+        def x_quant(q):
+            cols = slice(256 * q, 256 * (q + 1))
+            nc.vector.quantize_mx(
+                out=x_codes[:, cols].bitcast(FP8X4),
+                scales=x_planes[:, cols],
+                in_=state["xg", q][:].rearrange("p k t -> p (k t)"),
+            )
+
+        def mx_x(dst, n, codes, planes):
+            cols = slice(P * n, P * (n + 1))
+            nc.tensor.matmul_mx(
+                out=dst,
+                lhsT=x_codes[:, cols].bitcast(FP8X4),
+                lhsT_scale=x_planes[:, cols],
+                rhs=codes[:].bitcast(FP8X4),
+                rhs_scale=planes[:],
+                start=True,
+                stop=True,
+            )
+
+        def gate_matmul(q):
+            for s in range(2):
+                a_ps = psum.tile([P, D], F32, name="a_ps", tag="ub", bufs=4)
+                mx_x(a_ps[:], 2 * q + s, wg_codes, wg_planes)
+                state["a", 2 * q + s] = a_ps
+
+        def gate_silu(q):
+            for n in (2 * q, 2 * q + 1):
+                nc.scalar.activation(out=gate[:, n, :], in_=state["a", n][:], func=ACT.Silu)
+
+        NQ = NT // 2
+        for q in range(NQ + 5):
+            if 0 <= q - 4 < NQ:
+                gate_matmul(q - 4)
+            if 0 <= q - 1 < NQ:
+                x_transpose(q - 1)
+            if 0 <= q - 5 < NQ:
+                gate_silu(q - 5)
+            if 0 <= q - 2 < NQ:
+                x_copy(q - 2)
+            if q < NQ:
+                x_product(q)
+            if q == 2:
+                nc.vector.quantize_mx(
+                    out=wg_codes[:].bitcast(FP8X4),
+                    scales=wg_planes[:],
+                    in_=wg_il[:].rearrange("p c j -> p (c j)"),
+                )
+            for f in prep.get(q, []):
+                f()
+            if 0 <= q - 3 < NQ:
+                x_quant(q - 3)
+
+        def scores(n):
+            sc = psum.tile([P, C], F32, name="sc_ps", tag="sc", bufs=2)
+            mx_x(sc[:], n, wk_codes, wk_planes)
+            state["sc", n] = sc
+
+        def maxima(n):
+            nm = work.tile([P, 2 * H], F32, name="nm", bufs=3)
+            nc.vector.tensor_reduce(
+                out=nm[:],
+                in_=state["sc", n][:].rearrange("p (c k) -> p c k", k=N),
+                axis=AX.X,
+                op=ALU.max,
+                negate=True,
+            )
+            state["nm", n] = nm
+
+        def exps(n):
+            e = work.tile([P, 2, H, N], F32, name="e", bufs=4)
+            z = work.tile([P, 2 * H], F32, name="z", bufs=3)
+            sc, nm = state["sc", n], state["nm", n]
+            for half in range(2):
+                for h in range(H):
+                    c = 2 * h + half
+                    src = sc[:, N * c : N * (c + 1)]
+                    dst = e[:, half, h, :]
+                    if half == 1:
+                        src = src.rearrange("p (m t) -> p t m", t=4)
+                        dst = dst.rearrange("p (t m) -> p t m", t=4)
+                    nc.scalar.activation(
+                        out=dst,
+                        in_=src,
+                        func=ACT.Exp,
+                        bias=nm[:, c : c + 1],
+                        accum_out=z[:, H * half + h : H * half + h + 1],
+                    )
+            state["e", n], state["z", n] = e, z
+
+        def recips(n):
+            rz = work.tile([P, 2 * H], F32, name="rz", bufs=3)
+            nc.vector.reciprocal(out=rz[:], in_=state["z", n][:])
+            state["rz", n] = rz
+
+        def normalise(n):
+            rz = state["rz", n]
+            rr = work.tile([P, H], F32, name="rr", bufs=3)
+            nc.gpsimd.tensor_tensor(out=rr[:], in0=rz[:, 0:H], in1=rz[:, H : 2 * H], op=ALU.mult)
+            p1 = work.tile([P, H, N], F32, name="p1", bufs=3)
+            nc.gpsimd.tensor_tensor(
+                out=p1[:],
+                in0=state["e", n][:, 0, :, :],
+                in1=rr[:].unsqueeze(2).broadcast_to([P, H, N]),
+                op=ALU.mult,
+            )
+            state["p1", n] = p1
+
+        def p2_to_psum(n):
+            p2 = psum.tile([P, N], F32, name="p2_ps", tag="p2", bufs=1)
+            nc.tensor.matmul(
+                p2[:], lhsT=ident[:], rhs=state["e", n][:, 1, 0, :], start=True, stop=True
+            )
+            state["p2", n] = p2
+
+        def wide_product(eng, n, h, g, p2):
+            pr = work.tile([P, 4, P], F32, name="pr%d%d" % (h, g), bufs=2)
+            p1 = state["p1", n][:, h, 16 * g : 16 * (g + 1)]
+            eng.tensor_tensor(
+                out=pr[:].rearrange("p t (i m) -> p t i m", m=8),
+                in0=p1.unsqueeze(1).unsqueeze(3).broadcast_to([P, 4, 16, 8]),
+                in1=p2.rearrange("p (t m) -> p t m", t=4).unsqueeze(2).broadcast_to([P, 4, 16, 8]),
+                op=ALU.mult,
+            )
+            state["pr", n, h, g] = pr
+
+        def scalar_product(n, h, g):
+            pr = work.tile([P, 4, P], F32, name="pr%d%d" % (h, g), bufs=2)
+            for i in range(16):
+                ii = 16 * g + i
+                nc.scalar.activation(
+                    out=pr[:, :, 8 * i : 8 * (i + 1)],
+                    in_=state["e", n][:, 1, h, :].rearrange("p (t m) -> p t m", t=4),
+                    func=ACT.Copy,
+                    scale=state["p1", n][:, h, ii : ii + 1],
+                )
+            state["pr", n, h, g] = pr
+
+        def sum_heads(n, g):
+            ub = psum.tile([P, 4, P], F32, name="ub_ps", tag="ub", bufs=4)
+            for t in range(4):
+                for h in range(H):
+                    nc.tensor.matmul(
+                        ub[:, t, :],
+                        lhsT=state["pr", n, h, g][:, t, :],
+                        rhs=ident[:],
+                        start=(h == 0),
+                        stop=(h == H - 1),
+                        is_transpose=True,
+                    )
+            state["ub", n, g] = ub
+
+        def gain(n, g):
+            if g == 0:
+                u = work.tile([P, 2, P, 4], BF16, name="u", align_bytes=64)
+                state["u", n] = u
+            nc.vector.tensor_tensor(
+                out=state["u", n][:, g, :, :],
+                in0=state["ub", n, g][:].rearrange("p t k -> p k t"),
+                in1=gain_sb[:, g, :].unsqueeze(1).broadcast_to([P, P, 4]),
+                op=ALU.mult,
+            )
+
+        def u_quant(n):
+            uc = work.tile([P, 2 * P], U32, name="uc", align_bytes=64)
+            us = work.tile([P, 2 * P], U8, name="us", align_bytes=64)
+            nc.vector.quantize_mx(
+                out=uc[:].bitcast(FP8X4),
+                scales=us[:],
+                in_=state["u", n][:].rearrange("p g k t -> p (g k t)"),
+            )
+            state["uc", n] = (uc, us)
+
+        def memory(n):
+            mem = psum.tile([P, D], F32, name="mem", tag="mem", bufs=1)
+            uc, us = state["uc", n]
+            for g in range(2):
+                cols = slice(P * g, P * (g + 1))
+                nc.tensor.matmul_mx(
+                    out=mem[:],
+                    lhsT=uc[:, cols].bitcast(FP8X4),
+                    lhsT_scale=us[:, cols],
+                    rhs=v_codes[:, g, :].bitcast(FP8X4),
+                    rhs_scale=v_planes[:, g, :],
+                    start=(g == 0),
+                    stop=(g == 1),
+                )
+            state["mem", n] = mem
+
+        def final(n):
+            o = work.tile([P, D], F32, name="o", bufs=4)
+            nc.vector.tensor_tensor(
+                out=o[:], in0=state["mem", n][:], in1=gate[:, n, :], op=ALU.mult
+            )
+            nc.sync.dma_start(out=out_view[:, n, :], in_=o[:])
+
+        def has(n):
+            return 0 <= n < NT
+
+        for s in range(-4, NT + 3):
+            if has(s - 2):
+                memory(s - 2)
+            if has(s + 4):
+                scores(s + 4)
+            if has(s):
+                sum_heads(s, 0)
+            if has(s + 2):
+                p2_to_psum(s + 2)
+            if has(s):
+                sum_heads(s, 1)
+            if has(s + 3):
+                exps(s + 3)
+            if has(s + 1):
+                for h, g in S_UNITS:
+                    scalar_product(s + 1, h, g)
+            if has(s + 2):
+                recips(s + 2)
+            if has(s + 1):
+                for h, g in V_UNITS:
+                    wide_product(nc.vector, s + 1, h, g, state["p2", s + 1][:])
+            if has(s - 1):
+                gain(s - 1, 0)
+            if has(s - 2):
+                final(s - 2)
+            if has(s - 1):
+                gain(s - 1, 1)
+            if has(s + 4):
+                maxima(s + 4)
+            if has(s - 1):
+                u_quant(s - 1)
+            if has(s + 1):
+                wide_product(nc.gpsimd, s + 1, *G_UNITS[0], state["e", s + 1][:, 1, G_UNITS[0][0], :])
+            if has(s + 2):
+                normalise(s + 2)
+            if has(s + 1):
+                for h, g in G_UNITS[1:]:
+                    wide_product(nc.gpsimd, s + 1, h, g, state["e", s + 1][:, 1, h, :])

@@ -21,9 +21,9 @@ NT = T // P
 
 FLOPS = 2 * T * D * C + 2 * T * SLOTS * D + 2 * T * D * D
 
-V_UNITS = [(0, 0), (0, 1)]
-S_UNITS = [(1, 0), (1, 1), (2, 0)]
-G_UNITS = [(3, 0), (2, 1), (3, 1)]
+V_WHOLE, V_HALF = 0, (1, 0)
+S_UNITS = [(1, 1), (2, 0), (2, 1)]
+G_WHOLE = 3
 
 X_CHUNKS = [(0, 2), (2, 8), (8, 16), (16, 24), (24, 32)]
 
@@ -88,7 +88,6 @@ def tile_productkeysoftmemoryplus_t_kernel(
         gate = keep.tile([P, NT, D], F32, name="gate")
 
         wg_il = keep.tile([P, D, 4], BF16, name="wg_il", align_bytes=64)
-        nc.scalar.copy(out=wg_il[:], in_=wg_raw[:].rearrange("p j c -> p c j"))
 
         def wk_copy():
             wk_il = keep.tile([P, C, 4], BF16, name="wk_il", align_bytes=64)
@@ -121,10 +120,10 @@ def tile_productkeysoftmemoryplus_t_kernel(
             )
 
         state = {}
-        prep = {3: [wk_copy], 4: [wk_quant]}
+        prep = {5: [wk_copy], 6: [wk_quant]}
         for i in range(4):
-            prep.setdefault(6 + 2 * i, []).append(lambda i=i: v_copy(i))
-            prep.setdefault(7 + 2 * i, []).append(lambda i=i: v_quant(i))
+            prep.setdefault(7 + 2 * i, []).append(lambda i=i: v_copy(i))
+            prep.setdefault(8 + 2 * i, []).append(lambda i=i: v_quant(i))
 
         def x_product(q):
             xb = work.tile([P, 2, D], BF16, name="xb", align_bytes=64)
@@ -201,6 +200,8 @@ def tile_productkeysoftmemoryplus_t_kernel(
                 x_copy(q - 2)
             if q < NQ:
                 x_product(q)
+            if q == 1:
+                nc.vector.tensor_copy(out=wg_il[:], in_=wg_raw[:].rearrange("p j c -> p c j"))
             if q == 2:
                 nc.vector.quantize_mx(
                     out=wg_codes[:].bitcast(FP8X4),
@@ -255,47 +256,51 @@ def tile_productkeysoftmemoryplus_t_kernel(
             state["rz", n] = rz
 
         def normalise(n):
-            rz = state["rz", n]
-            rr = work.tile([P, H], F32, name="rr", bufs=3)
-            nc.gpsimd.tensor_tensor(out=rr[:], in0=rz[:, 0:H], in1=rz[:, H : 2 * H], op=ALU.mult)
-            p1 = work.tile([P, H, N], F32, name="p1", bufs=3)
+            pn = work.tile([P, 2, H, N], F32, name="pn", bufs=3)
             nc.gpsimd.tensor_tensor(
-                out=p1[:],
-                in0=state["e", n][:, 0, :, :],
-                in1=rr[:].unsqueeze(2).broadcast_to([P, H, N]),
+                out=pn[:].rearrange("p a h k -> p (a h) k"),
+                in0=state["e", n][:].rearrange("p a h k -> p (a h) k"),
+                in1=state["rz", n][:].unsqueeze(2).broadcast_to([P, 2 * H, N]),
                 op=ALU.mult,
             )
-            state["p1", n] = p1
+            state["pn", n] = pn
 
         def p2_to_psum(n):
-            p2 = psum.tile([P, N], F32, name="p2_ps", tag="p2", bufs=1)
+            p2 = psum.tile([P, 2, N], F32, name="p2_ps", tag="p2", bufs=1)
             nc.tensor.matmul(
-                p2[:], lhsT=ident[:], rhs=state["e", n][:, 1, 0, :], start=True, stop=True
+                p2[:].rearrange("p h k -> p (h k)"),
+                lhsT=ident[:],
+                rhs=state["pn", n][:, 1, 0:2, :].rearrange("p h k -> p (h k)"),
+                start=True,
+                stop=True,
             )
             state["p2", n] = p2
 
-        def wide_product(eng, n, h, g, p2):
-            pr = work.tile([P, 4, P], F32, name="pr%d%d" % (h, g), bufs=2)
-            p1 = state["p1", n][:, h, 16 * g : 16 * (g + 1)]
+        def wide_product(eng, n, h, lo, hi, p2):
+            ni = hi - lo
+            pr = work.tile([P, 4, ni * 8], F32, name="pr%d_%d" % (h, lo), bufs=2)
+            p1 = state["pn", n][:, 0, h, lo:hi]
             eng.tensor_tensor(
                 out=pr[:].rearrange("p t (i m) -> p t i m", m=8),
-                in0=p1.unsqueeze(1).unsqueeze(3).broadcast_to([P, 4, 16, 8]),
-                in1=p2.rearrange("p (t m) -> p t m", t=4).unsqueeze(2).broadcast_to([P, 4, 16, 8]),
+                in0=p1.unsqueeze(1).unsqueeze(3).broadcast_to([P, 4, ni, 8]),
+                in1=p2.rearrange("p (t m) -> p t m", t=4).unsqueeze(2).broadcast_to([P, 4, ni, 8]),
                 op=ALU.mult,
             )
-            state["pr", n, h, g] = pr
+            for g in range(lo // 16, hi // 16):
+                a = P * (g - lo // 16)
+                state["pr", n, h, g] = pr[:, :, a : a + P]
 
         def scalar_product(n, h, g):
-            pr = work.tile([P, 4, P], F32, name="pr%d%d" % (h, g), bufs=2)
+            pr = work.tile([P, 4, P], F32, name="pr%d_%d" % (h, 16 * g), bufs=2)
             for i in range(16):
                 ii = 16 * g + i
                 nc.scalar.activation(
                     out=pr[:, :, 8 * i : 8 * (i + 1)],
-                    in_=state["e", n][:, 1, h, :].rearrange("p (t m) -> p t m", t=4),
+                    in_=state["pn", n][:, 1, h, :].rearrange("p (t m) -> p t m", t=4),
                     func=ACT.Copy,
-                    scale=state["p1", n][:, h, ii : ii + 1],
+                    scale=state["pn", n][:, 0, h, ii : ii + 1],
                 )
-            state["pr", n, h, g] = pr
+            state["pr", n, h, g] = pr[:]
 
         def sum_heads(n, g):
             ub = psum.tile([P, 4, P], F32, name="ub_ps", tag="ub", bufs=4)
@@ -365,34 +370,31 @@ def tile_productkeysoftmemoryplus_t_kernel(
                 scores(s + 4)
             if has(s):
                 sum_heads(s, 0)
-            if has(s + 2):
-                p2_to_psum(s + 2)
-            if has(s):
                 sum_heads(s, 1)
+            if has(s + 2):
+                normalise(s + 2)
+                p2_to_psum(s + 2)
+            if has(s + 1):
+                wide_product(nc.gpsimd, s + 1, G_WHOLE, 0, N, state["pn", s + 1][:, 1, G_WHOLE, :])
             if has(s + 3):
                 exps(s + 3)
             if has(s + 1):
                 for h, g in S_UNITS:
                     scalar_product(s + 1, h, g)
-            if has(s + 2):
-                recips(s + 2)
-            if has(s + 1):
-                for h, g in V_UNITS:
-                    wide_product(nc.vector, s + 1, h, g, state["p2", s + 1][:])
             if has(s - 1):
                 gain(s - 1, 0)
-            if has(s - 2):
-                final(s - 2)
+            if has(s + 1):
+                wide_product(nc.vector, s + 1, V_WHOLE, 0, N, state["p2", s + 1][:, 0, :])
             if has(s - 1):
                 gain(s - 1, 1)
-            if has(s + 4):
-                maxima(s + 4)
+            if has(s - 2):
+                final(s - 2)
+            if has(s + 1):
+                h, g = V_HALF
+                wide_product(nc.vector, s + 1, h, 16 * g, 16 * (g + 1), state["p2", s + 1][:, 1, :])
             if has(s - 1):
                 u_quant(s - 1)
-            if has(s + 1):
-                wide_product(nc.gpsimd, s + 1, *G_UNITS[0], state["e", s + 1][:, 1, G_UNITS[0][0], :])
-            if has(s + 2):
-                normalise(s + 2)
-            if has(s + 1):
-                for h, g in G_UNITS[1:]:
-                    wide_product(nc.gpsimd, s + 1, h, g, state["e", s + 1][:, 1, h, :])
+            if has(s + 4):
+                maxima(s + 4)
+            if has(s + 3):
+                recips(s + 3)

@@ -21,9 +21,10 @@ NT = T // P
 
 FLOPS = 2 * T * D * C + 2 * T * SLOTS * D + 2 * T * D * D
 
-V_WHOLE, V_HALF = 0, (1, 0)
-S_UNITS = [(1, 1), (2, 0), (2, 1)]
+V_WHOLE = 0
 G_WHOLE = 3
+SHARED = (1, 0)
+S_HALVES = [(1, 1), (2, 0), (2, 1)]
 
 X_CHUNKS = [(0, 2), (2, 8), (8, 16), (16, 24), (24, 32)]
 
@@ -126,7 +127,7 @@ def tile_productkeysoftmemoryplus_t_kernel(
             prep.setdefault(8 + 2 * i, []).append(lambda i=i: v_quant(i))
 
         def x_product(q):
-            xb = work.tile([P, 2, D], BF16, name="xb", align_bytes=64)
+            xb = work.tile([P, 2, D], BF16, name="xb", bufs=3, align_bytes=64)
             for s in range(2):
                 n = 2 * q + s
                 i = [k for k, (a, b) in enumerate(X_CHUNKS) if a <= n < b][0]
@@ -149,7 +150,7 @@ def tile_productkeysoftmemoryplus_t_kernel(
             state["xt", q] = xt
 
         def x_copy(q):
-            xg = work.tile([P, 2 * P, 4], BF16, name="xg", align_bytes=64)
+            xg = work.tile([P, 2 * P, 4], BF16, name="xg", bufs=4, align_bytes=64)
             nc.scalar.copy(
                 out=xg[:].rearrange("p k t -> p (k t)").bitcast(F32).rearrange(
                     "p (s k u) -> p s k u", s=2, u=2
@@ -180,7 +181,7 @@ def tile_productkeysoftmemoryplus_t_kernel(
 
         def gate_matmul(q):
             for s in range(2):
-                a_ps = psum.tile([P, D], F32, name="a_ps", tag="ub", bufs=4)
+                a_ps = psum.tile([P, D], F32, name="a_ps", tag="ub", bufs=3)
                 mx_x(a_ps[:], 2 * q + s, wg_codes, wg_planes)
                 state["a", 2 * q + s] = a_ps
 
@@ -256,29 +257,31 @@ def tile_productkeysoftmemoryplus_t_kernel(
             state["rz", n] = rz
 
         def normalise(n):
-            pn = work.tile([P, 2, H, N], F32, name="pn", bufs=3)
+            if n % 2 == 0:
+                pn = work.tile([P, 2, 2 * H, N], F32, name="pn", bufs=3)
+                state["pn2", n // 2] = pn
+            pn = state["pn2", n // 2]
             nc.gpsimd.tensor_tensor(
-                out=pn[:].rearrange("p a h k -> p (a h) k"),
+                out=pn[:, n % 2, :, :],
                 in0=state["e", n][:].rearrange("p a h k -> p (a h) k"),
                 in1=state["rz", n][:].unsqueeze(2).broadcast_to([P, 2 * H, N]),
                 op=ALU.mult,
             )
-            state["pn", n] = pn
+            state["pn", n] = pn[:, n % 2, :, :].rearrange("p (a h) k -> p a h k", a=2)
 
-        def p2_to_psum(n):
-            p2 = psum.tile([P, 2, N], F32, name="p2_ps", tag="p2", bufs=1)
+        def p2_to_psum(q):
+            p2 = psum.tile([P, 2, 2, N], F32, name="p2_ps", tag="p2", bufs=2)
             nc.tensor.matmul(
-                p2[:].rearrange("p h k -> p (h k)"),
+                p2[:].rearrange("p s h k -> p s (h k)"),
                 lhsT=ident[:],
-                rhs=state["pn", n][:, 1, 0:2, :].rearrange("p h k -> p (h k)"),
+                rhs=state["pn2", q][:, :, H : H + 2, :].rearrange("p s h k -> p s (h k)"),
                 start=True,
                 stop=True,
             )
-            state["p2", n] = p2
+            state["p2", 2 * q], state["p2", 2 * q + 1] = p2[:, 0, :, :], p2[:, 1, :, :]
 
-        def wide_product(eng, n, h, lo, hi, p2):
+        def wide_product(eng, n, h, lo, hi, p2, pr):
             ni = hi - lo
-            pr = work.tile([P, 4, ni * 8], F32, name="pr%d_%d" % (h, lo), bufs=2)
             p1 = state["pn", n][:, 0, h, lo:hi]
             eng.tensor_tensor(
                 out=pr[:].rearrange("p t (i m) -> p t i m", m=8),
@@ -286,9 +289,17 @@ def tile_productkeysoftmemoryplus_t_kernel(
                 in1=p2.rearrange("p (t m) -> p t m", t=4).unsqueeze(2).broadcast_to([P, 4, ni, 8]),
                 op=ALU.mult,
             )
-            for g in range(lo // 16, hi // 16):
-                a = P * (g - lo // 16)
-                state["pr", n, h, g] = pr[:, :, a : a + P]
+
+        def whole_product(eng, n, h, p2):
+            pr = work.tile([P, 4, 2 * P], F32, name="pr%d" % h, bufs=2)
+            wide_product(eng, n, h, 0, N, p2, pr)
+            state["pr", n, h, 0] = pr[:, :, 0:P]
+            state["pr", n, h, 1] = pr[:, :, P : 2 * P]
+
+        def half_product(eng, n, h, g, p2):
+            pr = work.tile([P, 4, P], F32, name="pr%d_%d" % (h, 16 * g), bufs=2)
+            wide_product(eng, n, h, 16 * g, 16 * (g + 1), p2, pr)
+            state["pr", n, h, g] = pr[:]
 
         def scalar_product(n, h, g):
             pr = work.tile([P, 4, P], F32, name="pr%d_%d" % (h, 16 * g), bufs=2)
@@ -303,7 +314,7 @@ def tile_productkeysoftmemoryplus_t_kernel(
             state["pr", n, h, g] = pr[:]
 
         def sum_heads(n, g):
-            ub = psum.tile([P, 4, P], F32, name="ub_ps", tag="ub", bufs=4)
+            ub = psum.tile([P, 4, P], F32, name="ub_ps", tag="ub", bufs=3)
             for t in range(4):
                 for h in range(H):
                     nc.tensor.matmul(
@@ -363,38 +374,44 @@ def tile_productkeysoftmemoryplus_t_kernel(
         def has(n):
             return 0 <= n < NT
 
-        for s in range(-4, NT + 3):
+        def shared_on_scalar(n):
+            return n % 2 == 1
+
+        for s in range(-5, NT + 3):
             if has(s - 2):
                 memory(s - 2)
-            if has(s + 4):
-                scores(s + 4)
+            if has(s + 5):
+                scores(s + 5)
+            if has(s + 3):
+                normalise(s + 3)
+            if has(s + 1):
+                whole_product(nc.gpsimd, s + 1, G_WHOLE, state["pn", s + 1][:, 1, G_WHOLE, :])
             if has(s):
                 sum_heads(s, 0)
+            if s % 2 == 0 and has(s + 2):
+                p2_to_psum(s // 2 + 1)
+            if has(s):
                 sum_heads(s, 1)
-            if has(s + 2):
-                normalise(s + 2)
-                p2_to_psum(s + 2)
-            if has(s + 1):
-                wide_product(nc.gpsimd, s + 1, G_WHOLE, 0, N, state["pn", s + 1][:, 1, G_WHOLE, :])
-            if has(s + 3):
-                exps(s + 3)
-            if has(s + 1):
-                for h, g in S_UNITS:
-                    scalar_product(s + 1, h, g)
+            for k in range(3):
+                if has(s + 1):
+                    scalar_product(s + 1, *S_HALVES[k])
+                if k == 0 and has(s + 4):
+                    exps(s + 4)
+            if has(s + 1) and shared_on_scalar(s + 1):
+                scalar_product(s + 1, *SHARED)
             if has(s - 1):
                 gain(s - 1, 0)
             if has(s + 1):
-                wide_product(nc.vector, s + 1, V_WHOLE, 0, N, state["p2", s + 1][:, 0, :])
+                whole_product(nc.vector, s + 1, V_WHOLE, state["p2", s + 1][:, 0, :])
             if has(s - 1):
                 gain(s - 1, 1)
             if has(s - 2):
                 final(s - 2)
-            if has(s + 1):
-                h, g = V_HALF
-                wide_product(nc.vector, s + 1, h, 16 * g, 16 * (g + 1), state["p2", s + 1][:, 1, :])
+            if has(s + 1) and not shared_on_scalar(s + 1):
+                half_product(nc.vector, s + 1, *SHARED, state["p2", s + 1][:, 1, :])
             if has(s - 1):
                 u_quant(s - 1)
             if has(s + 4):
-                maxima(s + 4)
-            if has(s + 3):
-                recips(s + 3)
+                recips(s + 4)
+            if has(s + 5):
+                maxima(s + 5)

from contextlib import ExitStack

import concourse.mybir as mybir
from concourse.masks import make_identity

F32 = mybir.dt.float32
BF16 = mybir.dt.bfloat16
U32 = mybir.dt.uint32
U8 = mybir.dt.uint8
FP8 = mybir.dt.float8_e4m3fn
FP8X4 = mybir.dt.float8_e4m3fn_x4
ACT = mybir.ActivationFunctionType
ALU = mybir.AluOpType
AX = mybir.AxisListType

T, D, H, N = 4096, 512, 4, 32
C = H * 2 * N
SLOTS = N * N
P = 128
NT = T // P

FLOPS = 2 * T * D * C + 2 * T * SLOTS * D + 2 * T * D * D

V_WHOLE = 0
G_WHOLE = 3
SHARED = (1, 0)
S_HALVES = [(1, 1), (2, 0), (2, 1)]

X_CHUNKS = [(0, 2), (2, 8), (8, 16), (16, 24), (24, 32)]


def tile_productkeysoftmemoryplus_t_kernel(
    tc, x_bytes, x_scale, wk, slot_gain, values, wg, out
):
    nc = tc.nc
    x_view = x_bytes.rearrange("(p n) d -> p n d", n=NT)
    out_view = out.rearrange("(p n) d -> p n d", n=NT)

    with ExitStack() as ctx:
        keep = ctx.enter_context(tc.tile_pool(name="keep", bufs=1))
        work = ctx.enter_context(tc.tile_pool(name="work", bufs=2))
        psum = ctx.enter_context(tc.psum_pool(name="psum", bufs=1))
        ctx.enter_context(tc.manual_schedule())

        xraw = []
        for a, b in X_CHUNKS:
            xr = keep.tile([P, b - a, D], U8, name="xraw%d" % a, align_bytes=64)
            xraw.append(xr)
        scale_sb = keep.tile([P, D], F32, name="scale_sb")
        wg_raw = keep.tile([P, 4, D], BF16, name="wg_raw")
        wk_raw = keep.tile([P, 4, C], BF16, name="wk_raw")
        v_raw = keep.tile([P, 2, 4, D], BF16, name="v_raw")
        gain_sb = keep.tile([P, 2, 4], BF16, name="gain_sb")

        def load_x(i):
            a, b = X_CHUNKS[i]
            nc.sync.dma_start(out=xraw[i][:], in_=x_view[:, a:b, :])

        nc.sync.dma_start(out=scale_sb[:], in_=x_scale.rearrange("o k -> (o k)").partition_broadcast(P))
        load_x(0)
        nc.sync.dma_start(out=wg_raw[:], in_=wg.rearrange("(p j) c -> p j c", j=4))
        load_x(1)
        nc.sync.dma_start(out=wk_raw[:], in_=wk.rearrange("(p j) c -> p j c", j=4))
        load_x(2)
        for g in range(2):
            nc.sync.dma_start(
                out=v_raw[:, g, :, :],
                in_=values[512 * g : 512 * (g + 1), :].rearrange("(p j) c -> p j c", j=4),
            )
        nc.sync.dma_start(out=gain_sb[:], in_=slot_gain.rearrange("(g p t) -> p g t", p=P, t=4))
        load_x(3)
        load_x(4)

        ident = keep.tile([P, P], F32, name="ident")
        make_identity(nc, ident[:])
        warm = keep.tile([P, 1], F32, name="warm")
        nc.gpsimd.memset(warm[:], 0.0)
        warm_out = keep.tile([P, 1], F32, name="warm_out")
        nc.scalar.activation(out=warm_out[:], in_=warm[:], func=ACT.Silu)

        x_codes = keep.tile([P, T], U32, name="x_codes", align_bytes=64)
        x_planes = keep.tile([P, T], U8, name="x_planes", align_bytes=64)
        wg_codes = keep.tile([P, D], U32, name="wg_codes", align_bytes=64)
        wg_planes = keep.tile([P, D], U8, name="wg_planes", align_bytes=64)
        wk_codes = keep.tile([P, C], U32, name="wk_codes", align_bytes=64)
        wk_planes = keep.tile([P, C], U8, name="wk_planes", align_bytes=64)
        v_codes = keep.tile([P, 2, D], U32, name="v_codes", align_bytes=64)
        v_planes = keep.tile([P, 2, D], U8, name="v_planes", align_bytes=64)
        gate = keep.tile([P, NT, D], F32, name="gate")

        wg_il = keep.tile([P, D, 4], BF16, name="wg_il", align_bytes=64)

        def wk_copy():
            wk_il = keep.tile([P, C, 4], BF16, name="wk_il", align_bytes=64)
            nc.vector.tensor_copy(out=wk_il[:], in_=wk_raw[:].rearrange("p j c -> p c j"))
            state["wk_il"] = wk_il

        def wk_quant():
            nc.vector.quantize_mx(
                out=wk_codes[:].bitcast(FP8X4),
                scales=wk_planes[:],
                in_=state["wk_il"][:].rearrange("p c j -> p (c j)"),
            )

        def v_copy(i):
            g, b = divmod(i, 2)
            v_il = work.tile([P, 256, 4], BF16, name="v_il", align_bytes=64)
            nc.vector.tensor_copy(
                out=v_il[:],
                in_=v_raw[:, g, :, 256 * b : 256 * (b + 1)].rearrange("p j c -> p c j"),
            )
            state["v_il", i] = v_il

        def v_quant(i):
            g, b = divmod(i, 2)
            cols = slice(256 * b, 256 * (b + 1))
            nc.vector.quantize_mx(
                out=v_codes[:, g, cols].bitcast(FP8X4),
                scales=v_planes[:, g, cols],
                in_=state["v_il", i][:].rearrange("p c j -> p (c j)"),
            )

        state = {}
        prep = {5: [wk_copy], 6: [wk_quant]}
        for i in range(4):
            prep.setdefault(7 + 2 * i, []).append(lambda i=i: v_copy(i))
            prep.setdefault(8 + 2 * i, []).append(lambda i=i: v_quant(i))

        def x_product(q):
            xb = work.tile([P, 2, D], BF16, name="xb", bufs=3, align_bytes=64)
            for s in range(2):
                n = 2 * q + s
                i = [k for k, (a, b) in enumerate(X_CHUNKS) if a <= n < b][0]
                nc.vector.tensor_tensor(
                    out=xb[:, s, :],
                    in0=xraw[i][:, n - X_CHUNKS[i][0], :].bitcast(FP8),
                    in1=scale_sb[:],
                    op=ALU.mult,
                )
            state["xb", q] = xb

        def x_transpose(q):
            words = state["xb", q][:].rearrange("p s d -> p (s d)").bitcast(F32)
            xt = psum.tile([P, 2, 2, P], F32, name="xt", tag="sc", bufs=2)
            for s in range(2):
                for u in range(2):
                    nc.tensor.transpose(
                        xt[:, s, u, :], words[:, 256 * s + u : 256 * (s + 1) : 2], ident[:]
                    )
            state["xt", q] = xt

        def x_copy(q):
            xg = work.tile([P, 2 * P, 4], BF16, name="xg", bufs=4, align_bytes=64)
            nc.scalar.copy(
                out=xg[:].rearrange("p k t -> p (k t)").bitcast(F32).rearrange(
                    "p (s k u) -> p s k u", s=2, u=2
                ),
                in_=state["xt", q][:].rearrange("p s u k -> p s k u"),
            )
            state["xg", q] = xg

        def x_quant(q):
            cols = slice(256 * q, 256 * (q + 1))
            nc.vector.quantize_mx(
                out=x_codes[:, cols].bitcast(FP8X4),
                scales=x_planes[:, cols],
                in_=state["xg", q][:].rearrange("p k t -> p (k t)"),
            )

        def mx_x(dst, n, codes, planes):
            cols = slice(P * n, P * (n + 1))
            nc.tensor.matmul_mx(
                out=dst,
                lhsT=x_codes[:, cols].bitcast(FP8X4),
                lhsT_scale=x_planes[:, cols],
                rhs=codes[:].bitcast(FP8X4),
                rhs_scale=planes[:],
                start=True,
                stop=True,
            )

        def gate_matmul(q):
            for s in range(2):
                a_ps = psum.tile([P, D], F32, name="a_ps", tag="ub", bufs=3)
                mx_x(a_ps[:], 2 * q + s, wg_codes, wg_planes)
                state["a", 2 * q + s] = a_ps

        def gate_silu(q):
            for n in (2 * q, 2 * q + 1):
                nc.scalar.activation(out=gate[:, n, :], in_=state["a", n][:], func=ACT.Silu)

        NQ = NT // 2
        for q in range(NQ + 5):
            if 0 <= q - 4 < NQ:
                gate_matmul(q - 4)
            if 0 <= q - 1 < NQ:
                x_transpose(q - 1)
            if 0 <= q - 5 < NQ:
                gate_silu(q - 5)
            if 0 <= q - 2 < NQ:
                x_copy(q - 2)
            if q < NQ:
                x_product(q)
            if q == 1:
                nc.vector.tensor_copy(out=wg_il[:], in_=wg_raw[:].rearrange("p j c -> p c j"))
            if q == 2:
                nc.vector.quantize_mx(
                    out=wg_codes[:].bitcast(FP8X4),
                    scales=wg_planes[:],
                    in_=wg_il[:].rearrange("p c j -> p (c j)"),
                )
            for f in prep.get(q, []):
                f()
            if 0 <= q - 3 < NQ:
                x_quant(q - 3)

        def scores(n):
            sc = psum.tile([P, C], F32, name="sc_ps", tag="sc", bufs=2)
            mx_x(sc[:], n, wk_codes, wk_planes)
            state["sc", n] = sc

        def maxima(n):
            nm = work.tile([P, 2 * H], F32, name="nm", bufs=3)
            nc.vector.tensor_reduce(
                out=nm[:],
                in_=state["sc", n][:].rearrange("p (c k) -> p c k", k=N),
                axis=AX.X,
                op=ALU.max,
                negate=True,
            )
            state["nm", n] = nm

        def exps(n):
            e = work.tile([P, 2, H, N], F32, name="e", bufs=4)
            z = work.tile([P, 2 * H], F32, name="z", bufs=3)
            sc, nm = state["sc", n], state["nm", n]
            for half in range(2):
                for h in range(H):
                    c = 2 * h + half
                    src = sc[:, N * c : N * (c + 1)]
                    dst = e[:, half, h, :]
                    if half == 1:
                        src = src.rearrange("p (m t) -> p t m", t=4)
                        dst = dst.rearrange("p (t m) -> p t m", t=4)
                    nc.scalar.activation(
                        out=dst,
                        in_=src,
                        func=ACT.Exp,
                        bias=nm[:, c : c + 1],
                        accum_out=z[:, H * half + h : H * half + h + 1],
                    )
            state["e", n], state["z", n] = e, z

        def recips(n):
            rz = work.tile([P, 2 * H], F32, name="rz", bufs=3)
            nc.vector.reciprocal(out=rz[:], in_=state["z", n][:])
            state["rz", n] = rz

        def normalise(n):
            if n % 2 == 0:
                pn = work.tile([P, 2, 2 * H, N], F32, name="pn", bufs=3)
                state["pn2", n // 2] = pn
            pn = state["pn2", n // 2]
            nc.gpsimd.tensor_tensor(
                out=pn[:, n % 2, :, :],
                in0=state["e", n][:].rearrange("p a h k -> p (a h) k"),
                in1=state["rz", n][:].unsqueeze(2).broadcast_to([P, 2 * H, N]),
                op=ALU.mult,
            )
            state["pn", n] = pn[:, n % 2, :, :].rearrange("p (a h) k -> p a h k", a=2)

        def p2_to_psum(q):
            p2 = psum.tile([P, 2, 2, N], F32, name="p2_ps", tag="p2", bufs=2)
            nc.tensor.matmul(
                p2[:].rearrange("p s h k -> p s (h k)"),
                lhsT=ident[:],
                rhs=state["pn2", q][:, :, H : H + 2, :].rearrange("p s h k -> p s (h k)"),
                start=True,
                stop=True,
            )
            state["p2", 2 * q], state["p2", 2 * q + 1] = p2[:, 0, :, :], p2[:, 1, :, :]

        def wide_product(eng, n, h, lo, hi, p2, pr):
            ni = hi - lo
            p1 = state["pn", n][:, 0, h, lo:hi]
            eng.tensor_tensor(
                out=pr[:].rearrange("p t (i m) -> p t i m", m=8),
                in0=p1.unsqueeze(1).unsqueeze(3).broadcast_to([P, 4, ni, 8]),
                in1=p2.rearrange("p (t m) -> p t m", t=4).unsqueeze(2).broadcast_to([P, 4, ni, 8]),
                op=ALU.mult,
            )

        def whole_product(eng, n, h, p2):
            pr = work.tile([P, 4, 2 * P], F32, name="pr%d" % h, bufs=2)
            wide_product(eng, n, h, 0, N, p2, pr)
            state["pr", n, h, 0] = pr[:, :, 0:P]
            state["pr", n, h, 1] = pr[:, :, P : 2 * P]

        def half_product(eng, n, h, g, p2):
            pr = work.tile([P, 4, P], F32, name="pr%d_%d" % (h, 16 * g), bufs=2)
            wide_product(eng, n, h, 16 * g, 16 * (g + 1), p2, pr)
            state["pr", n, h, g] = pr[:]

        def scalar_product(n, h, g):
            pr = work.tile([P, 4, P], F32, name="pr%d_%d" % (h, 16 * g), bufs=2)
            for i in range(16):
                ii = 16 * g + i
                nc.scalar.activation(
                    out=pr[:, :, 8 * i : 8 * (i + 1)],
                    in_=state["pn", n][:, 1, h, :].rearrange("p (t m) -> p t m", t=4),
                    func=ACT.Copy,
                    scale=state["pn", n][:, 0, h, ii : ii + 1],
                )
            state["pr", n, h, g] = pr[:]

        def sum_heads(n, g):
            ub = psum.tile([P, 4, P], F32, name="ub_ps", tag="ub", bufs=3)
            for t in range(4):
                for h in range(H):
                    nc.tensor.matmul(
                        ub[:, t, :],
                        lhsT=state["pr", n, h, g][:, t, :],
                        rhs=ident[:],
                        start=(h == 0),
                        stop=(h == H - 1),
                        is_transpose=True,
                    )
            state["ub", n, g] = ub

        def gain(n, g):
            if g == 0:
                u = work.tile([P, 2, P, 4], BF16, name="u", align_bytes=64)
                state["u", n] = u
            nc.vector.tensor_tensor(
                out=state["u", n][:, g, :, :],
                in0=state["ub", n, g][:].rearrange("p t k -> p k t"),
                in1=gain_sb[:, g, :].unsqueeze(1).broadcast_to([P, P, 4]),
                op=ALU.mult,
            )

        def u_quant(n):
            uc = work.tile([P, 2 * P], U32, name="uc", align_bytes=64)
            us = work.tile([P, 2 * P], U8, name="us", align_bytes=64)
            nc.vector.quantize_mx(
                out=uc[:].bitcast(FP8X4),
                scales=us[:],
                in_=state["u", n][:].rearrange("p g k t -> p (g k t)"),
            )
            state["uc", n] = (uc, us)

        def memory(n):
            mem = psum.tile([P, D], F32, name="mem", tag="mem", bufs=1)
            uc, us = state["uc", n]
            for g in range(2):
                cols = slice(P * g, P * (g + 1))
                nc.tensor.matmul_mx(
                    out=mem[:],
                    lhsT=uc[:, cols].bitcast(FP8X4),
                    lhsT_scale=us[:, cols],
                    rhs=v_codes[:, g, :].bitcast(FP8X4),
                    rhs_scale=v_planes[:, g, :],
                    start=(g == 0),
                    stop=(g == 1),
                )
            state["mem", n] = mem

        def final(n):
            o = work.tile([P, D], F32, name="o", bufs=4)
            nc.vector.tensor_tensor(
                out=o[:], in0=state["mem", n][:], in1=gate[:, n, :], op=ALU.mult
            )
            nc.sync.dma_start(out=out_view[:, n, :], in_=o[:])

        def has(n):
            return 0 <= n < NT

        def shared_on_scalar(n):
            return n % 2 == 1

        for s in range(-5, NT + 3):
            if has(s - 2):
                memory(s - 2)
            if has(s + 5):
                scores(s + 5)
            if has(s + 3):
                normalise(s + 3)
            if has(s + 1):
                whole_product(nc.gpsimd, s + 1, G_WHOLE, state["pn", s + 1][:, 1, G_WHOLE, :])
            if has(s):
                sum_heads(s, 0)
            if s % 2 == 0 and has(s + 2):
                p2_to_psum(s // 2 + 1)
            if has(s):
                sum_heads(s, 1)
            for k in range(3):
                if has(s + 1):
                    scalar_product(s + 1, *S_HALVES[k])
                if k == 0 and has(s + 4):
                    exps(s + 4)
            if has(s + 1) and shared_on_scalar(s + 1):
                scalar_product(s + 1, *SHARED)
            if has(s - 1):
                gain(s - 1, 0)
            if has(s + 1):
                whole_product(nc.vector, s + 1, V_WHOLE, state["p2", s + 1][:, 0, :])
            if has(s - 1):
                gain(s - 1, 1)
            if has(s - 2):
                final(s - 2)
            if has(s + 1) and not shared_on_scalar(s + 1):
                half_product(nc.vector, s + 1, *SHARED, state["p2", s + 1][:, 1, :])
            if has(s - 1):
                u_quant(s - 1)
            if has(s + 4):
                recips(s + 4)
            if has(s + 5):
                maxima(s + 5)
